import numpy as np
import ml_dtypes


def mxq(x, axis, fmt="e4m3"):
    dtype, down = {"e4m3": (ml_dtypes.float8_e4m3fn, 7), "e5m2": (ml_dtypes.float8_e5m2, 14)}[fmt]
    v = np.moveaxis(np.asarray(x, np.float32).astype(ml_dtypes.bfloat16).astype(np.float64), axis, -1)
    blocks = v.reshape(v.shape[:-1] + (-1, 32))
    amax = np.abs(blocks).max(-1, keepdims=True)
    byte = np.maximum(np.where(amax > 0, np.frexp(amax)[1] - 1 + 127, 0) - down, 1)
    scale = np.exp2(byte - 127.0)
    codes = (blocks / scale).astype(np.float32).astype(dtype).astype(np.float64)
    return np.moveaxis((codes * scale).reshape(v.shape), -1, axis)


WIDE = False


def mx_kscale(k):
    if not WIDE:
        return np.ones(k)
    levels = np.array([10, -10, 5, -5, 0])
    if k % 512:
        return np.exp2(np.random.permutation(np.resize(levels, k // 32))).repeat(32)
    a = np.empty((k // 512, 16))
    for p in range(k // 512):
        a[p, :8] = np.random.permutation(np.resize(levels, 8))
        for g in range(8):
            far = levels[np.abs(levels - a[p, g]) >= 10]
            a[p, g + 8] = far[np.random.randint(len(far))]
    return np.exp2(a.ravel()).repeat(32)


def f64(x):
    return np.asarray(x).astype(np.float64)


def striped(idx):
    return np.tile(idx.reshape(-1, 16).T, (8, 1)).astype(np.uint16)


def unstriped(offs):
    return offs[:16].T.reshape(-1).astype(np.int64)


def pack_weight(w):
    k, n = w.shape
    w = f64(np.asarray(w, np.float32).astype(ml_dtypes.bfloat16)).reshape(k // 32, 32, n)
    amax = np.abs(w).max(1)
    byte = np.clip(np.where(amax > 0, np.frexp(amax)[1] - 1 + 127 - 7, 1), 1, 254)
    scaled = (w * np.exp2(127.0 - byte)[:, None, :]).reshape(k, n).astype(np.float32)
    words = np.ascontiguousarray(scaled.reshape(k // 512, 128, 4, n).transpose(0, 1, 3, 2)).astype(ml_dtypes.float8_e4m3fn).view(np.uint8)
    return words, np.ascontiguousarray(byte.astype(np.uint8).reshape(k // 512, 16, n))


def unpack_weight(words, scales):
    g, p, n, _ = words.shape
    vals = np.ascontiguousarray(words).view(ml_dtypes.float8_e4m3fn).astype(np.float64) * np.repeat(np.exp2(scales.astype(np.float64) - 127.0), 8, axis=1)[..., None]
    return vals.transpose(0, 1, 3, 2).reshape(g * 512, n)


E2M1 = np.array([0.0, 0.5, 1.0, 1.5, 2.0, 3.0, 4.0, 6.0, -0.0, -0.5, -1.0, -1.5, -2.0, -3.0, -4.0, -6.0])


def pack_fp4(w):
    k, n = w.shape
    w = f64(np.asarray(w, np.float32).astype(ml_dtypes.bfloat16)).reshape(k // 32, 32, n)
    amax = np.abs(w).max(1)
    mant, ex = np.frexp(amax / 6.0)
    byte = np.clip(np.where(amax > 0, np.where(mant > 0.5, ex, ex - 1) + 127, 1), 1, 254)
    scaled = (w * np.exp2(127.0 - byte)[:, None, :]).reshape(k, n).astype(np.float32)
    c = np.ascontiguousarray(scaled.reshape(k // 512, 128, 4, n).transpose(0, 1, 3, 2)).astype(ml_dtypes.float4_e2m1fn).view(np.uint8) & 0xF
    words = (c[..., 0::2] | (c[..., 1::2] << 4)).reshape(k // 512, 128, 2 * n)
    return np.ascontiguousarray(words), np.ascontiguousarray(byte.astype(np.uint8).reshape(k // 512, 16, n))


def unpack_fp4(words, scales):
    g, _, n = scales.shape
    words = np.ascontiguousarray(words).reshape(g, 128, n, 2)
    nib = np.empty((g, 128, n, 4), np.uint8)
    nib[..., 0::2] = words & 0xF
    nib[..., 1::2] = words >> 4
    vals = E2M1[nib] * np.repeat(np.exp2(scales.astype(np.float64) - 127.0), 8, axis=1)[..., None]
    return vals.transpose(0, 1, 3, 2).reshape(g * 512, n)


def sigmoid(v):
    return 1.0 / (1.0 + np.exp(-np.maximum(v, -700.0)))


K, T, S, D, N, H, V, U = 512, 4096, 1024, 4, 256, 512, 256, 512


def setup_inputs():
    n = np.random.standard_normal
    s = mx_kscale(K)[:, None]
    u = mx_kscale(H)
    packed_xT = pack_weight(n((K, T)) * s)
    packed_w1 = pack_fp4(n((K, H)) / np.sqrt(K) / s)
    packed_w2 = pack_fp4(n((K, H)) / np.sqrt(K) / s)
    packed_w3 = pack_fp4(n((H, N)) / np.sqrt(H) / u[:, None])
    return {
        "x_words": packed_xT[0],
        "x_scales": packed_xT[1],
        "w1_words": packed_w1[0],
        "w1_scales": packed_w1[1],
        "w2_words": packed_w2[0],
        "w2_scales": packed_w2[1],
        "cnt": (np.random.uniform(-2.0, 2.0, (H, U))).astype(np.float32),
        "idv": (n((H, U))).astype(np.float32),
        "unit": (np.random.uniform(0.6, 1.4, (H, 1)) * u[:, None]).astype(np.float32),
        "w3_words": packed_w3[0],
        "w3_scales": packed_w3[1],
        "offs": striped(np.random.permutation(T)[:S]),
        "new": striped(np.random.permutation(np.concatenate([np.arange(V), np.random.randint(0, V, U - V)]))),
    }


def reference(x_words, x_scales, w1_words, w1_scales, w2_words, w2_scales, cnt, idv, unit, w3_words, w3_scales, offs, new):
    warm = sigmoid(f64(cnt))
    xq = unpack_weight(x_words, x_scales)[:, unstriped(offs)]
    ys = unpack_fp4(w2_words, w2_scales).T @ xq
    prtop = ys.reshape(len(ys), -1, D).max(axis=2)
    prexp = np.exp(ys - np.repeat(prtop, D, axis=1))
    prsum = prexp.reshape(len(prexp), -1, D).sum(axis=2)
    pr = prexp / np.repeat(prsum, D, axis=1)
    y = unpack_fp4(w1_words, w1_scales).T @ xq
    wy = pr * y
    agg = wy.reshape(len(wy), -1, D).sum(axis=2)
    mn = agg[:, unstriped(new)]
    mixd = warm * f64(idv) + (-1.0 * warm + 1.0) * mn
    wv = pr * ((y - np.repeat(agg, D, axis=1)) ** 2)
    spread = wv.reshape(len(wv), -1, D).sum(axis=2)
    hid = f64(unit) * (mixd / (np.sqrt(spread[:, unstriped(new)] + 0.1) + 0.5))
    return unpack_fp4(w3_words, w3_scales).T @ mxq(hid, 0, "e4m3")

@@ -1,0 +1,361 @@
+from contextlib import ExitStack
+
+import concourse.mybir as mybir
+from concourse.masks import make_identity
+
+K, T, S, D, N, H, V, U = 512, 4096, 1024, 4, 256, 512, 256, 512
+FLOPS = 2 * K * H * S * 2 + 2 * H * N * U
+
+F32 = mybir.dt.float32
+BF16 = mybir.dt.bfloat16
+I32 = mybir.dt.int32
+U32 = mybir.dt.uint32
+U16 = mybir.dt.uint16
+U8 = mybir.dt.uint8
+FP8X4 = mybir.dt.float8_e4m3fn_x4
+FP4X4 = mybir.dt.float4_e2m1fn_x4
+ALU = mybir.AluOpType
+ACT = mybir.ActivationFunctionType
+AX = mybir.AxisListType
+
+P = 128
+PACK = 4
+HALVES = V // P
+WINDOW = V + 16
+MN = "SSSSSSSS"
+PART = "GVVV"
+INV = "SSSSSSSV"
+MIX = "GVVV"
+BIG = 4
+RING = 3
+ORD = 2
+WEAVE = "VV"
+YLAG = 4
+TH = 1
+KEPT = 2
+EARLY = 1
+INVB = 8
+
+
+def load_scales(queues, plane, rows):
+    for q, queue in enumerate(queues):
+        queue.dma_start(out=plane[32 * q : 32 * q + 4, :].bitcast(I32), in_=rows[4 * q : 4 * q + 4, :].bitcast(I32))
+
+
+def deal_words(nc, words, raw):
+    nc.scalar.copy(
+        out=words[:].bitcast(U16).rearrange("p (t m) -> p t m", t=PACK),
+        in_=raw[:].bitcast(U16).rearrange("p (m t) -> p t m", t=PACK),
+    )
+
+
+def deal_scales(engine, scales, raw):
+    engine.tensor_copy(
+        out=scales[:].rearrange("p (t m) -> p t m", t=PACK),
+        in_=raw[:].rearrange("p (m t) -> p t m", t=PACK),
+    )
+
+
+def tile_picked_ycoldb_rel_p_kernel(
+    tc, x_words, x_scales, w1_words, w1_scales, w2_words, w2_scales, cnt, idv, unit, w3_words, w3_scales, offs, new, out
+):
+    nc = tc.nc
+    with ExitStack() as ctx:
+        keep = ctx.enter_context(tc.tile_pool(name="keep", bufs=1))
+        ring = ctx.enter_context(tc.tile_pool(name="ring", bufs=RING))
+        big = ctx.enter_context(tc.psum_pool(name="big", bufs=BIG))
+        sum_banks = ctx.enter_context(tc.psum_pool(name="sum_banks", bufs=8 - BIG))
+
+        def sb(name, shape, dtype, tag=None):
+            return keep.tile(shape, dtype, name=name, tag=tag or name, align_bytes=64)
+
+        offs_t = sb("offs_t", [P, S // 16], U16)
+        new_t = sb("new_t", [P, U // 16], U16)
+        xw = sb("xw", [P, T], U32)
+        xs = sb("xs", [P, T], U8)
+        w_raw = [sb("w_raw0", [P, 2 * H], U8, tag="idv_t"), sb("w_raw1", [P, 2 * H], U8, tag="cnt_t")]
+        ws_raw = sb("ws_raw1", [P, H], U8, tag="raw_scales")
+        w_words = [sb("w_words%d" % a, [P, 2 * H], U8) for a in range(2)]
+        w_scales = [sb("w_scales%d" % a, [P, H], U8) for a in range(2)]
+        w3w = sb("w3w", [P, 2 * N], U8)
+        unit_t = sb("unit_t", [P, PACK], F32)
+        ident = sb("ident", [P, P], F32)
+
+        nc.vector.memset(xs[:].bitcast(I32), 0)
+        nc.vector.memset(ws_raw[:].bitcast(I32), 0)
+        nc.sync.dma_start(offs_t[:], offs)
+        nc.sync.dma_start(new_t[:], new)
+        nc.sync.dma_start(out=w_raw[1][:].bitcast(I32), in_=w2_words[0].bitcast(I32))
+        nc.sync.dma_start(out=xw[:].bitcast(I32), in_=x_words[0].rearrange("p c r -> p (c r)").bitcast(I32))
+        load_scales([nc.scalar] * 4, xs, x_scales[0])
+        load_scales([nc.gpsimd, nc.scalar, nc.scalar, nc.scalar], ws_raw, w2_scales[0])
+        nc.gpsimd.dma_start(out=w_raw[0][:].bitcast(I32), in_=w1_words[0].bitcast(I32))
+        make_identity(nc, ident[:])
+        nc.gpsimd.dma_start(out=unit_t[:], in_=unit.rearrange("(p t) o -> p (t o)", t=PACK))
+        nc.gpsimd.dma_start(out=w3w[:].bitcast(I32), in_=w3_words[0].bitcast(I32))
+
+        agg_win = [sb("agg_win%d" % t, [P, WINDOW], F32) for t in range(PACK)]
+        inv_win = [sb("inv_win%d" % t, [P, WINDOW], F32) for t in range(PACK)]
+        for t in range(PACK):
+            nc.gpsimd.memset(agg_win[t][:, V:], 0.0)
+            nc.gpsimd.memset(inv_win[t][:, V:], 0.0)
+
+        x_cols = S // HALVES
+        xq_words, xq_scales = [], []
+        for h in range(HALVES):
+            entries = offs_t[:, h * x_cols // 16 : (h + 1) * x_cols // 16]
+            got = sb("got_s%d" % h, [P, x_cols], U8, tag="got%d" % h)
+            nc.vector.tensor_copy(got[:], xs[:].indirect(entries))
+            dealt = sb("xq_s%d" % h, [P, D, P], U8)
+            nc.vector.tensor_copy(out=dealt[:], in_=got[:].rearrange("p (v d) -> p d v", d=D))
+            xq_scales.append(dealt)
+
+        deal_words(nc, w_words[1], w_raw[1])
+        deal_words(nc, w_words[0], w_raw[0])
+        deal_scales(nc.vector, w_scales[1], ws_raw)
+        cnt_t = sb("cnt_t", [P, PACK, U], F32)
+        idv_t = sb("idv_t", [P, PACK, U], F32)
+        nc.sync.dma_start(out=cnt_t[:], in_=cnt.rearrange("(p t) r -> p t r", t=PACK))
+        nc.sync.dma_start(out=idv_t[:], in_=idv.rearrange("(p t) r -> p t r", t=PACK))
+        ws_raw = sb("ws_raw0", [P, H], U8, tag="raw_scales")
+        nc.gpsimd.memset(ws_raw[:].bitcast(I32), 0)
+        load_scales([nc.sync] * 4, ws_raw, w1_scales[0])
+        deal_scales(nc.gpsimd, w_scales[0], ws_raw)
+        w3s = sb("w3s", [P, N], U8, tag="raw_scales")
+        nc.gpsimd.memset(w3s[:].bitcast(I32), 0)
+        load_scales([nc.sync] * 4, w3s, w3_scales[0])
+
+        def gather_words(h):
+            entries = offs_t[:, h * x_cols // 16 : (h + 1) * x_cols // 16]
+            got = sb("got_w%d" % h, [P, x_cols], U32, tag="got1")
+            nc.vector.tensor_copy(got[:], xw[:].indirect(entries))
+            dealt = sb("xq_w%d" % h, [P, D, P], U32)
+            nc.vector.tensor_copy(out=dealt[:], in_=got[:].rearrange("p (v d) -> p d v", d=D))
+            xq_words.append(dealt)
+
+        def product(a, t, h):
+            bank = big.tile([P, D, P], F32, name="bank")
+            for d in range(D):
+                nc.tensor.matmul_mx(
+                    out=bank[:, d, :],
+                    lhsT=xq_words[h][:, d, :].bitcast(FP8X4),
+                    lhsT_scale=xq_scales[h][:, d, :],
+                    rhs=w_words[a][:, 2 * P * t : 2 * P * (t + 1)].bitcast(FP4X4),
+                    rhs_scale=w_scales[a][:, P * t : P * (t + 1)],
+                    start=True,
+                    stop=True,
+                )
+            return bank
+
+        def sum_over_d(dst, planes):
+            for d in range(D):
+                nc.tensor.matmul(dst, lhsT=planes[:, d, :], rhs=ident[:], start=(d == 0), stop=(d == D - 1), is_transpose=True)
+
+        def over_d(plane):
+            return plane.unsqueeze(1).to_broadcast([P, D, P])
+
+        units = [(t, h) for h in range(HALVES) for t in range(PACK)]
+        total = [sum_banks.tile([P, 2, V], F32, name="sums") for a in range(2)]
+        first = [sum_banks.tile([P, 2, V], F32, name="sums") for a in range(2)]
+        th = sb("th", [P, PACK, U], F32)
+        cold2 = sb("cold2", [P, PACK, U], F32)
+        own2 = sb("own2", [P, PACK, U], F32)
+        expo, score, top, diff, feat, held = {}, {}, {}, {}, {}, {}
+
+        def score_max(u):
+            score[u] = product(1, *u)
+            top[u] = ring.tile([P, P], F32, name="top")
+            nc.vector.tensor_reduce(out=top[u][:], in_=score[u][:].rearrange("p d i -> p i d"), axis=AX.X, op=ALU.max)
+
+        def score_exp(u):
+            t, h = u
+            diff[u] = sb("last_diff", [P, D, P], F32) if u == units[-1] else ring.tile([P, D, P], F32, name="diff")
+            nc.vector.tensor_tensor(out=diff[u][:], in0=score[u][:], in1=over_d(top[u][:]), op=ALU.subtract)
+            expo[u] = sb("expo%d%d" % u, [P, D, P], F32)
+            nc.scalar.activation(out=expo[u][:], in_=diff[u][:], func=ACT.Exp)
+            sum_over_d(total[t // 2][:, t % 2, h * P : (h + 1) * P], expo[u])
+
+        def weigh(u):
+            t, h = u
+            bank = product(0, t, h)
+            wy = ring.tile([P, D, P], F32, name="wy")
+            nc.vector.tensor_tensor(out=wy[:], in0=bank[:], in1=expo[u][:], op=ALU.mult)
+            feat[u] = sb("feat%d%d" % u, [P, D, P], F32)
+            if t < KEPT:
+                nc.scalar.copy(out=feat[u][:], in_=bank[:])
+            else:
+                held[u] = bank
+            sum_over_d(first[t // 2][:, t % 2, h * P : (h + 1) * P], wy)
+
+        order = sorted(units, key=lambda u: (u[0] // 2, u[1] if u[0] < 2 else u[0], u[0], u[1]))
+        gather_words(0)
+        score_max(units[0])
+        for n, u in enumerate(units):
+            if n == 1:
+                gather_words(1)
+            if n + 1 < len(units):
+                score_max(units[n + 1])
+            score_exp(u)
+            if n >= YLAG:
+                weigh(order[n - YLAG])
+            if n >= TH and n < TH + PACK:
+                t = n - TH
+                nc.scalar.activation(out=th[:, t, :], in_=cnt_t[:, t, :], func=ACT.Tanh, scale=0.5)
+                nc.gpsimd.tensor_scalar(out=cold2[:, t, :], in0=th[:, t, :], scalar1=-1.0, scalar2=1.0, op0=ALU.mult, op1=ALU.add)
+                warm2 = ring.tile([P, U], F32, name="warm2")
+                nc.gpsimd.tensor_scalar(out=warm2[:], in0=th[:, t, :], scalar1=1.0, scalar2=1.0, op0=ALU.mult, op1=ALU.add)
+                nc.gpsimd.tensor_tensor(out=own2[:, t, :], in0=warm2[:], in1=idv_t[:, t, :], op=ALU.mult)
+        squared = sb("squared", [P, PACK, V], F32)
+        for a in range(2):
+            nc.scalar.activation(out=squared[:, 2 * a : 2 * a + 2, :], in_=total[a][:], func=ACT.Square)
+        last = diff[units[-1]][:].rearrange("p d i -> p (d i)")
+        other = sb("inv_total", [P, 2 * V], F32)
+        inv_total = [last[:, :V], last[:, V:], other[:, :V], other[:, V:]]
+        for t in range(PACK):
+            nc.scalar.activation(out=inv_total[t], in_=squared[:, t, :], func=ACT.Abs_reciprocal_sqrt)
+        for u in order[len(units) - YLAG :]:
+            weigh(u)
+        half = U // 2
+        hid = [sb("hid%d" % c, [P, PACK, half], BF16) for c in range(2)]
+        turned, spread, mix = {}, {}, {}
+
+        def centre(t):
+            nc.vector.tensor_tensor(out=agg_win[t][:, :V], in0=first[t // 2][:, t % 2, :], in1=inv_total[t], op=ALU.mult)
+            if t % 2 == 0:
+                turned[t // 2] = sum_banks.tile([P, 2, V], F32, name="sums")
+            for h in range(HALVES):
+                nc.tensor.transpose(turned[t // 2][:, t % 2, h * P : (h + 1) * P], agg_win[t][:, h * P : (h + 1) * P], ident[:])
+
+        def deviate(t):
+            means = turned[t // 2][:, t % 2, :]
+            if t >= KEPT:
+                copied = ring.tile([P, V], F32, name="copied")
+                nc.scalar.copy(out=copied[:], in_=means)
+                means = copied[:]
+            for h in range(HALVES):
+                dev = feat[t, h][:]
+                nc.vector.tensor_tensor(
+                    out=dev, in0=dev if t < KEPT else held[t, h][:], in1=over_d(means[:, h * P : (h + 1) * P]), op=ALU.subtract
+                )
+                nc.scalar.activation(out=dev, in_=dev, func=ACT.Square)
+
+        def spread_sum(t):
+            spread[t] = sum_banks.tile([P, 2, V], F32, name="sums") if t < 2 else big.tile([P, 2, V], F32, name="bank")
+            for h in range(HALVES):
+                wv = feat[t, h]
+                nc.vector.scalar_tensor_tensor(out=wv[:], in0=wv[:], scalar=0.1, in1=expo[t, h][:], op0=ALU.add, op1=ALU.mult)
+                sum_over_d(spread[t][:, 0, h * P : (h + 1) * P], wv)
+
+        def look_up(engine, dst, window, c):
+            entries = new_t[:, c * half // 16 : (c + 1) * half // 16]
+            if engine == "S":
+                nc.scalar.activation(dst, window[:].indirect(entries), ACT.Copy)
+            else:
+                nc.vector.tensor_copy(dst, window[:].indirect(entries))
+
+        def blend(t):
+            mn = ring.tile([P, U], F32, name="mn")
+            for c in range(2):
+                look_up(MN[2 * t + c], mn[:, c * half : (c + 1) * half], agg_win[t], c)
+            part = ring.tile([P, U], F32, name="part")
+            (nc.vector if PART[t] == "V" else nc.gpsimd).tensor_tensor(out=part[:], in0=mn[:], in1=cold2[:, t, :], op=ALU.mult)
+            mix[t] = sb("mix%d" % t, [P, U], F32)
+            (nc.vector if MIX[t] == "V" else nc.gpsimd).tensor_tensor(out=mix[t][:], in0=part[:], in1=own2[:, t, :], op=ALU.add)
+
+        def finish(t):
+            var = ring.tile([P, V], F32, name="var")
+            nc.vector.tensor_tensor(out=var[:], in0=spread[t][:, 0, :], in1=inv_total[t], op=ALU.mult)
+            rs = ring.tile([P, V], F32, name="rs")
+            nc.scalar.activation(out=rs[:], in_=var[:], func=ACT.Abs_reciprocal_sqrt)
+            quarter = ring.tile([P, V], F32, name="quarter")
+            nc.vector.scalar_tensor_tensor(out=quarter[:], in0=rs[:], scalar=1.0, in1=var[:], op0=ALU.add, op1=ALU.mult)
+            nc.scalar.activation(out=inv_win[t][:, :V], in_=quarter[:], func=ACT.Abs_reciprocal_sqrt, scale=4.0, bias=1.0)
+
+        def scale(t):
+            for c in range(2):
+                cols = slice(c * half, (c + 1) * half)
+                inv = ring.tile([P, half], F32, name="inv", bufs=INVB)
+                look_up(INV[2 * t + c], inv[:], inv_win[t], c)
+                nc.vector.scalar_tensor_tensor(
+                    out=hid[c][:, t, :], in0=mix[t][:, cols], scalar=unit_t[:, t : t + 1], in1=inv[:], op0=ALU.mult, op1=ALU.mult
+                )
+
+        for t in range(PACK):
+            centre(t)
+        if ORD == 0:
+            for t in range(EARLY):
+                blend(t)
+            for t in range(PACK):
+                deviate(t)
+            for t in range(PACK):
+                spread_sum(t)
+                finish(t)
+            for t in range(EARLY, PACK):
+                blend(t)
+            for t in range(PACK):
+                scale(t)
+        if ORD == 1:
+            for t in range(PACK):
+                deviate(t)
+                if t < EARLY:
+                    blend(t)
+            for t in range(PACK):
+                spread_sum(t)
+                finish(t)
+            for t in range(EARLY, PACK):
+                blend(t)
+            for t in range(PACK):
+                scale(t)
+        if ORD == 2:
+            for t in range(PACK):
+                deviate(t)
+                if t < EARLY:
+                    blend(t)
+            for t in range(PACK + 1):
+                if t < PACK:
+                    spread_sum(t)
+                if t > 0:
+                    finish(t - 1)
+            for t in range(PACK):
+                if t >= EARLY:
+                    blend(t)
+                scale(t)
+        if ORD == 3:
+            for t in range(PACK + 2):
+                if t < PACK:
+                    deviate(t)
+                if t < EARLY:
+                    blend(t)
+                if 0 <= t - 1 < PACK:
+                    spread_sum(t - 1)
+                if 0 <= t - 2 < PACK:
+                    finish(t - 2)
+            for t in range(PACK):
+                if t >= EARLY:
+                    blend(t)
+                scale(t)
+
+        for c in range(2):
+            cols = slice(c * half, (c + 1) * half)
+            woven = sb("woven%d" % c, [P, half, PACK], BF16)
+            if WEAVE[c] == "V":
+                nc.vector.tensor_copy(out=woven[:], in_=hid[c][:].rearrange("p t r -> p r t"))
+            else:
+                nc.scalar.copy(out=woven[:], in_=hid[c][:].rearrange("p t r -> p r t"))
+            codes = sb("codes%d" % c, [P, half], U32)
+            scales = sb("scales%d" % c, [P, half], U8)
+            nc.vector.quantize_mx(out=codes[:].bitcast(FP8X4), scales=scales[:], in_=woven[:].rearrange("p r t -> p (r t)"))
+            bank = big.tile([P, 2, half], F32, name="bank")
+            for m in range(N // P):
+                nc.tensor.matmul_mx(
+                    out=bank[:, m, :],
+                    lhsT=w3w[:, 2 * P * m : 2 * P * (m + 1)].bitcast(FP4X4),
+                    lhsT_scale=w3s[:, P * m : P * (m + 1)],
+                    rhs=codes[:].bitcast(FP8X4),
+                    rhs_scale=scales[:],
+                    start=True,
+                    stop=True,
+                )
+            res = sb("res%d" % c, [P, 2, half], F32)
+            nc.scalar.copy(out=res[:], in_=bank[:])
+            nc.sync.dma_start(out=out[:, cols].rearrange("(m p) r -> p m r", p=P), in_=res[:])

@@ -22,19 +22,20 @@ P = 128
 PACK = 4
 HALVES = V // P
 WINDOW = V + 16
-MN = "SSSSSSSS"
-PART = "GVVV"
-INV = "SSSSSSSV"
-MIX = "GVVV"
-BIG = 4
+SQE = "GGGGVVVV"
+MN = "SSFF"
+PART = "VVVV"
+MIX = "VVVV"
+INV = "SSSSSSSS"
+RES = "SV"
+XSPLIT = 4
+TH = 0
+ORD = 1
 RING = 3
-ORD = 2
-WEAVE = "VV"
-YLAG = 4
-TH = 1
-KEPT = 2
-EARLY = 1
-INVB = 8
+CEN = 0
+EARLY = [2, 3]
+SQ = 4
+AFTER = [-1, 3, 6, 7]
 
 
 def load_scales(queues, plane, rows):
@@ -63,292 +64,274 @@ def tile_picked_ycoldb_rel_p_kernel(
     with ExitStack() as ctx:
         keep = ctx.enter_context(tc.tile_pool(name="keep", bufs=1))
         ring = ctx.enter_context(tc.tile_pool(name="ring", bufs=RING))
-        big = ctx.enter_context(tc.psum_pool(name="big", bufs=BIG))
-        sum_banks = ctx.enter_context(tc.psum_pool(name="sum_banks", bufs=8 - BIG))
+        big = ctx.enter_context(tc.psum_pool(name="big", bufs=3))
+        hold = ctx.enter_context(tc.psum_pool(name="hold", bufs=2))
+        sum_banks = ctx.enter_context(tc.psum_pool(name="sum_banks", bufs=3))
 
         def sb(name, shape, dtype, tag=None):
             return keep.tile(shape, dtype, name=name, tag=tag or name, align_bytes=64)
+
+        def pick(letter):
+            return nc.vector if letter == "V" else nc.gpsimd
 
         offs_t = sb("offs_t", [P, S // 16], U16)
         new_t = sb("new_t", [P, U // 16], U16)
         xw = sb("xw", [P, T], U32)
         xs = sb("xs", [P, T], U8)
-        w_raw = [sb("w_raw0", [P, 2 * H], U8, tag="idv_t"), sb("w_raw1", [P, 2 * H], U8, tag="cnt_t")]
-        ws_raw = sb("ws_raw1", [P, H], U8, tag="raw_scales")
+        w_raw = [sb("w_raw0", [P, 2 * H], U8, tag="w3w"), sb("w_raw1", [P, 2 * H], U8, tag="cnt_t")]
+        ws_raw = [sb("ws_raw0", [P, H], U8), sb("ws_raw1", [P, H], U8, tag="idv_t")]
         w_words = [sb("w_words%d" % a, [P, 2 * H], U8) for a in range(2)]
         w_scales = [sb("w_scales%d" % a, [P, H], U8) for a in range(2)]
-        w3w = sb("w3w", [P, 2 * N], U8)
+        w3s = sb("w3s", [P, N], U8)
         unit_t = sb("unit_t", [P, PACK], F32)
         ident = sb("ident", [P, P], F32)
 
         nc.vector.memset(xs[:].bitcast(I32), 0)
-        nc.vector.memset(ws_raw[:].bitcast(I32), 0)
+        nc.vector.memset(ws_raw[1][:].bitcast(I32), 0)
         nc.sync.dma_start(offs_t[:], offs)
         nc.sync.dma_start(new_t[:], new)
         nc.sync.dma_start(out=w_raw[1][:].bitcast(I32), in_=w2_words[0].bitcast(I32))
         nc.sync.dma_start(out=xw[:].bitcast(I32), in_=x_words[0].rearrange("p c r -> p (c r)").bitcast(I32))
         load_scales([nc.scalar] * 4, xs, x_scales[0])
-        load_scales([nc.gpsimd, nc.scalar, nc.scalar, nc.scalar], ws_raw, w2_scales[0])
+        load_scales([nc.gpsimd, nc.scalar, nc.scalar, nc.scalar], ws_raw[1], w2_scales[0])
+        nc.vector.memset(ws_raw[0][:].bitcast(I32), 0)
+        nc.vector.memset(w3s[:].bitcast(I32), 0)
+        deal_words(nc, w_words[1], w_raw[1])
+        deal_scales(nc.gpsimd, w_scales[1], ws_raw[1])
         nc.gpsimd.dma_start(out=w_raw[0][:].bitcast(I32), in_=w1_words[0].bitcast(I32))
-        make_identity(nc, ident[:])
         nc.gpsimd.dma_start(out=unit_t[:], in_=unit.rearrange("(p t) o -> p (t o)", t=PACK))
-        nc.gpsimd.dma_start(out=w3w[:].bitcast(I32), in_=w3_words[0].bitcast(I32))
+        make_identity(nc, ident[:])
 
-        agg_win = [sb("agg_win%d" % t, [P, WINDOW], F32) for t in range(PACK)]
+        x_cols = S // HALVES
+        xq_scales = [sb("xq_scales%d" % h, [P, x_cols], U8)[:] for h in range(HALVES)]
+
+        def gather(dst, table, h):
+            nc.vector.tensor_copy(dst[h], table[:].indirect(offs_t[:, h * x_cols // 16 : (h + 1) * x_cols // 16]))
+
+        for h in range(HALVES):
+            gather(xq_scales, xs, h)
+        picked = sb("picked", [P, HALVES, x_cols], U32, tag="xs")
+        xq_words = [picked[:, h, :] for h in range(HALVES)]
+        cnt_t = sb("cnt_t", [P, PACK, U], F32)
+        idv_t = sb("idv_t", [P, PACK, U], F32)
+        nc.sync.dma_start(out=cnt_t[:], in_=cnt.rearrange("(p t) r -> p t r", t=PACK))
+        load_scales([nc.sync] * 4, ws_raw[0], w1_scales[0])
+        nc.sync.dma_start(out=idv_t[:], in_=idv.rearrange("(p t) r -> p t r", t=PACK))
+        deal_words(nc, w_words[0], w_raw[0])
+        deal_scales(nc.gpsimd, w_scales[0], ws_raw[0])
+        w3w = sb("w3w", [P, 2 * N], U8)
+        nc.sync.dma_start(out=w3w[:].bitcast(I32), in_=w3_words[0].bitcast(I32))
+        load_scales([nc.sync] * 4, w3s, w3_scales[0])
+
+        agg_win = [sb("agg_win%d" % t, [P, U + 16], F32) for t in range(PACK)]
         inv_win = [sb("inv_win%d" % t, [P, WINDOW], F32) for t in range(PACK)]
         for t in range(PACK):
             nc.gpsimd.memset(agg_win[t][:, V:], 0.0)
             nc.gpsimd.memset(inv_win[t][:, V:], 0.0)
 
-        x_cols = S // HALVES
-        xq_words, xq_scales = [], []
-        for h in range(HALVES):
-            entries = offs_t[:, h * x_cols // 16 : (h + 1) * x_cols // 16]
-            got = sb("got_s%d" % h, [P, x_cols], U8, tag="got%d" % h)
-            nc.vector.tensor_copy(got[:], xs[:].indirect(entries))
-            dealt = sb("xq_s%d" % h, [P, D, P], U8)
-            nc.vector.tensor_copy(out=dealt[:], in_=got[:].rearrange("p (v d) -> p d v", d=D))
-            xq_scales.append(dealt)
-
-        deal_words(nc, w_words[1], w_raw[1])
-        deal_words(nc, w_words[0], w_raw[0])
-        deal_scales(nc.vector, w_scales[1], ws_raw)
-        cnt_t = sb("cnt_t", [P, PACK, U], F32)
-        idv_t = sb("idv_t", [P, PACK, U], F32)
-        nc.sync.dma_start(out=cnt_t[:], in_=cnt.rearrange("(p t) r -> p t r", t=PACK))
-        nc.sync.dma_start(out=idv_t[:], in_=idv.rearrange("(p t) r -> p t r", t=PACK))
-        ws_raw = sb("ws_raw0", [P, H], U8, tag="raw_scales")
-        nc.gpsimd.memset(ws_raw[:].bitcast(I32), 0)
-        load_scales([nc.sync] * 4, ws_raw, w1_scales[0])
-        deal_scales(nc.gpsimd, w_scales[0], ws_raw)
-        w3s = sb("w3s", [P, N], U8, tag="raw_scales")
-        nc.gpsimd.memset(w3s[:].bitcast(I32), 0)
-        load_scales([nc.sync] * 4, w3s, w3_scales[0])
-
-        def gather_words(h):
-            entries = offs_t[:, h * x_cols // 16 : (h + 1) * x_cols // 16]
-            got = sb("got_w%d" % h, [P, x_cols], U32, tag="got1")
-            nc.vector.tensor_copy(got[:], xw[:].indirect(entries))
-            dealt = sb("xq_w%d" % h, [P, D, P], U32)
-            nc.vector.tensor_copy(out=dealt[:], in_=got[:].rearrange("p (v d) -> p d v", d=D))
-            xq_words.append(dealt)
-
-        def product(a, t, h):
-            bank = big.tile([P, D, P], F32, name="bank")
-            for d in range(D):
-                nc.tensor.matmul_mx(
-                    out=bank[:, d, :],
-                    lhsT=xq_words[h][:, d, :].bitcast(FP8X4),
-                    lhsT_scale=xq_scales[h][:, d, :],
-                    rhs=w_words[a][:, 2 * P * t : 2 * P * (t + 1)].bitcast(FP4X4),
-                    rhs_scale=w_scales[a][:, P * t : P * (t + 1)],
-                    start=True,
-                    stop=True,
-                )
+        def product(a, t, h, pool=big):
+            bank = pool.tile([P, P, D], F32, name="bank")
+            nc.tensor.matmul_mx(
+                out=bank[:].rearrange("p v d -> p (v d)"),
+                lhsT=w_words[a][:, 2 * P * t : 2 * P * (t + 1)].bitcast(FP4X4),
+                lhsT_scale=w_scales[a][:, P * t : P * (t + 1)],
+                rhs=xq_words[h].bitcast(FP8X4),
+                rhs_scale=xq_scales[h],
+                start=True,
+                stop=True,
+            )
             return bank
 
+        def planes_of(bank):
+            return bank[:].rearrange("p v d -> p d v")
+
+        def turned_sum(dst, terms):
+            for n, term in enumerate(terms):
+                nc.tensor.matmul(dst, lhsT=term, rhs=ident[:], start=(n == 0), stop=(n == len(terms) - 1), is_transpose=True)
+
         def sum_over_d(dst, planes):
-            for d in range(D):
-                nc.tensor.matmul(dst, lhsT=planes[:, d, :], rhs=ident[:], start=(d == 0), stop=(d == D - 1), is_transpose=True)
+            turned_sum(dst, [planes[:, d, :] for d in range(D)])
 
         def over_d(plane):
             return plane.unsqueeze(1).to_broadcast([P, D, P])
 
-        units = [(t, h) for h in range(HALVES) for t in range(PACK)]
+        def block(h):
+            return slice(h * P, (h + 1) * P)
+
+        units = [(t, h) for t in range(PACK) for h in range(HALVES)]
         total = [sum_banks.tile([P, 2, V], F32, name="sums") for a in range(2)]
-        first = [sum_banks.tile([P, 2, V], F32, name="sums") for a in range(2)]
-        th = sb("th", [P, PACK, U], F32)
+        first = {}
         cold2 = sb("cold2", [P, PACK, U], F32)
         own2 = sb("own2", [P, PACK, U], F32)
-        expo, score, top, diff, feat, held = {}, {}, {}, {}, {}, {}
+        expo, score, top, diff, feat, held, th = {}, {}, {}, {}, {}, {}, {}
 
         def score_max(u):
             score[u] = product(1, *u)
             top[u] = ring.tile([P, P], F32, name="top")
-            nc.vector.tensor_reduce(out=top[u][:], in_=score[u][:].rearrange("p d i -> p i d"), axis=AX.X, op=ALU.max)
+            nc.vector.tensor_reduce(out=top[u][:], in_=score[u][:], axis=AX.X, op=ALU.max)
 
         def score_exp(u):
             t, h = u
-            diff[u] = sb("last_diff", [P, D, P], F32) if u == units[-1] else ring.tile([P, D, P], F32, name="diff")
-            nc.vector.tensor_tensor(out=diff[u][:], in0=score[u][:], in1=over_d(top[u][:]), op=ALU.subtract)
+            diff[u] = sb("diff%d%d" % u, [P, D, P], F32)
+            nc.vector.tensor_tensor(out=diff[u][:], in0=planes_of(score[u]), in1=over_d(top[u][:]), op=ALU.subtract)
             expo[u] = sb("expo%d%d" % u, [P, D, P], F32)
             nc.scalar.activation(out=expo[u][:], in_=diff[u][:], func=ACT.Exp)
-            sum_over_d(total[t // 2][:, t % 2, h * P : (h + 1) * P], expo[u])
+            sum_over_d(total[t // 2][:, t % 2, block(h)], expo[u])
 
         def weigh(u):
             t, h = u
-            bank = product(0, t, h)
-            wy = ring.tile([P, D, P], F32, name="wy")
-            nc.vector.tensor_tensor(out=wy[:], in0=bank[:], in1=expo[u][:], op=ALU.mult)
+            if t % 2 == 0 and h == 0:
+                first[t // 2] = sum_banks.tile([P, 2, V], F32, name="sums")
+            held[u] = product(0, t, h, hold if t == 0 else big)
             feat[u] = sb("feat%d%d" % u, [P, D, P], F32)
-            if t < KEPT:
-                nc.scalar.copy(out=feat[u][:], in_=bank[:])
-            else:
-                held[u] = bank
-            sum_over_d(first[t // 2][:, t % 2, h * P : (h + 1) * P], wy)
+            nc.vector.tensor_tensor(out=feat[u][:], in0=planes_of(held[u]), in1=expo[u][:], op=ALU.mult)
+            sum_over_d(first[t // 2][:, t % 2, block(h)], feat[u])
 
-        order = sorted(units, key=lambda u: (u[0] // 2, u[1] if u[0] < 2 else u[0], u[0], u[1]))
-        gather_words(0)
+        minus_unit = sb("minus_unit", [P, PACK], F32)
+        nc.gpsimd.tensor_scalar(out=minus_unit[:], in0=unit_t[:], scalar1=-1.0, scalar2=0.0, op0=ALU.mult, op1=ALU.add)
+        gather(xq_words, xw, 0)
+        gather(xq_words, xw, 1)
+        squared = sb("squared", [P, PACK, V], F32)
+        early = EARLY
         score_max(units[0])
         for n, u in enumerate(units):
-            if n == 1:
-                gather_words(1)
             if n + 1 < len(units):
                 score_max(units[n + 1])
             score_exp(u)
-            if n >= YLAG:
-                weigh(order[n - YLAG])
+            if n in early:
+                weigh(units[early.index(n)])
+            if n == SQ:
+                nc.scalar.activation(out=squared[:, :2, :], in_=total[0][:], func=ACT.Square)
             if n >= TH and n < TH + PACK:
                 t = n - TH
-                nc.scalar.activation(out=th[:, t, :], in_=cnt_t[:, t, :], func=ACT.Tanh, scale=0.5)
-                nc.gpsimd.tensor_scalar(out=cold2[:, t, :], in0=th[:, t, :], scalar1=-1.0, scalar2=1.0, op0=ALU.mult, op1=ALU.add)
-                warm2 = ring.tile([P, U], F32, name="warm2")
-                nc.gpsimd.tensor_scalar(out=warm2[:], in0=th[:, t, :], scalar1=1.0, scalar2=1.0, op0=ALU.mult, op1=ALU.add)
-                nc.gpsimd.tensor_tensor(out=own2[:, t, :], in0=warm2[:], in1=idv_t[:, t, :], op=ALU.mult)
-        squared = sb("squared", [P, PACK, V], F32)
-        for a in range(2):
-            nc.scalar.activation(out=squared[:, 2 * a : 2 * a + 2, :], in_=total[a][:], func=ACT.Square)
-        last = diff[units[-1]][:].rearrange("p d i -> p (d i)")
-        other = sb("inv_total", [P, 2 * V], F32)
-        inv_total = [last[:, :V], last[:, V:], other[:, :V], other[:, V:]]
+                th[t] = diff[units[n]][:].rearrange("p d v -> p (d v)")
+                nc.scalar.activation(out=th[t], in_=cnt_t[:, t, :], func=ACT.Tanh, scale=0.5)
         for t in range(PACK):
-            nc.scalar.activation(out=inv_total[t], in_=squared[:, t, :], func=ACT.Abs_reciprocal_sqrt)
-        for u in order[len(units) - YLAG :]:
+            gain = unit_t[:, t : t + 1]
+            nc.gpsimd.tensor_scalar(
+                out=cold2[:, t, :], in0=th[t], scalar1=minus_unit[:, t : t + 1], scalar2=gain, op0=ALU.mult, op1=ALU.add
+            )
+            nc.gpsimd.tensor_scalar(out=th[t], in0=th[t], scalar1=gain, scalar2=gain, op0=ALU.mult, op1=ALU.add)
+            nc.gpsimd.tensor_tensor(out=own2[:, t, :], in0=th[t], in1=idv_t[:, t, :], op=ALU.mult)
+        inv_total = [diff[u][:].rearrange("p (a b) v -> p a (b v)", a=2) for u in (units[-1], units[-2])]
+        nc.scalar.activation(out=squared[:, 2:, :], in_=total[1][:], func=ACT.Square)
+        for a in range(2):
+            nc.scalar.activation(out=inv_total[a], in_=squared[:, 2 * a : 2 * a + 2, :], func=ACT.Abs_reciprocal_sqrt)
+        for u in units[len(early) :]:
             weigh(u)
         half = U // 2
-        hid = [sb("hid%d" % c, [P, PACK, half], BF16) for c in range(2)]
-        turned, spread, mix = {}, {}, {}
+        looked = [sb("looked%d" % c, [P, PACK, half], F32) for c in range(2)]
+        mix = sb("mix", [P, PACK, U], F32)
+        spread, square = {}, {}
 
-        def centre(t):
-            nc.vector.tensor_tensor(out=agg_win[t][:, :V], in0=first[t // 2][:, t % 2, :], in1=inv_total[t], op=ALU.mult)
-            if t % 2 == 0:
-                turned[t // 2] = sum_banks.tile([P, 2, V], F32, name="sums")
-            for h in range(HALVES):
-                nc.tensor.transpose(turned[t // 2][:, t % 2, h * P : (h + 1) * P], agg_win[t][:, h * P : (h + 1) * P], ident[:])
+        def centre(a):
+            mean = ring.tile([P, 2, V], F32, name="mean")
+            nc.vector.tensor_tensor(out=mean[:], in0=first[a][:], in1=inv_total[a], op=ALU.mult)
+            turned = sum_banks.tile([P, 2, V], F32, name="sums")
+            for b in range(2):
+                for h in range(HALVES):
+                    turned_sum(turned[:, b, block(h)], [mean[:, b, block(h)]])
+            for b in range(2):
+                nc.scalar.copy(out=agg_win[2 * a + b][:, :V], in_=turned[:, b, :])
 
         def deviate(t):
-            means = turned[t // 2][:, t % 2, :]
-            if t >= KEPT:
-                copied = ring.tile([P, V], F32, name="copied")
-                nc.scalar.copy(out=copied[:], in_=means)
-                means = copied[:]
             for h in range(HALVES):
+                bank = held[t, h] if t in (0, 3) else product(0, t, h, big if (t, h) == (2, 0) else hold)
                 dev = feat[t, h][:]
-                nc.vector.tensor_tensor(
-                    out=dev, in0=dev if t < KEPT else held[t, h][:], in1=over_d(means[:, h * P : (h + 1) * P]), op=ALU.subtract
-                )
-                nc.scalar.activation(out=dev, in_=dev, func=ACT.Square)
+                nc.vector.tensor_tensor(out=dev, in0=planes_of(bank), in1=over_d(agg_win[t][:, block(h)]), op=ALU.subtract)
+                square[t, h] = sb("square%d%d" % (t, h), [P, D, P], F32)
+                nc.scalar.activation(out=square[t, h][:], in_=dev, func=ACT.Square)
 
-        def spread_sum(t):
-            spread[t] = sum_banks.tile([P, 2, V], F32, name="sums") if t < 2 else big.tile([P, 2, V], F32, name="bank")
+        def spread_sum(t, n):
+            spread[t] = sum_banks.tile([P, 2, V], F32, name="sums")
             for h in range(HALVES):
-                wv = feat[t, h]
-                nc.vector.scalar_tensor_tensor(out=wv[:], in0=wv[:], scalar=0.1, in1=expo[t, h][:], op0=ALU.add, op1=ALU.mult)
-                sum_over_d(spread[t][:, 0, h * P : (h + 1) * P], wv)
-
-        def look_up(engine, dst, window, c):
-            entries = new_t[:, c * half // 16 : (c + 1) * half // 16]
-            if engine == "S":
-                nc.scalar.activation(dst, window[:].indirect(entries), ACT.Copy)
-            else:
-                nc.vector.tensor_copy(dst, window[:].indirect(entries))
-
-        def blend(t):
-            mn = ring.tile([P, U], F32, name="mn")
-            for c in range(2):
-                look_up(MN[2 * t + c], mn[:, c * half : (c + 1) * half], agg_win[t], c)
-            part = ring.tile([P, U], F32, name="part")
-            (nc.vector if PART[t] == "V" else nc.gpsimd).tensor_tensor(out=part[:], in0=mn[:], in1=cold2[:, t, :], op=ALU.mult)
-            mix[t] = sb("mix%d" % t, [P, U], F32)
-            (nc.vector if MIX[t] == "V" else nc.gpsimd).tensor_tensor(out=mix[t][:], in0=part[:], in1=own2[:, t, :], op=ALU.add)
+                wv = square[t, h]
+                pick(SQE[2 * n + h]).tensor_tensor(out=wv[:], in0=wv[:], in1=expo[t, h][:], op=ALU.mult)
+                sum_over_d(spread[t][:, 0, block(h)], wv)
 
         def finish(t):
             var = ring.tile([P, V], F32, name="var")
-            nc.vector.tensor_tensor(out=var[:], in0=spread[t][:, 0, :], in1=inv_total[t], op=ALU.mult)
+            nc.vector.tensor_tensor(out=var[:], in0=spread[t][:, 0, :], in1=inv_total[t // 2][:, t % 2, :], op=ALU.mult)
             rs = ring.tile([P, V], F32, name="rs")
-            nc.scalar.activation(out=rs[:], in_=var[:], func=ACT.Abs_reciprocal_sqrt)
-            quarter = ring.tile([P, V], F32, name="quarter")
-            nc.vector.scalar_tensor_tensor(out=quarter[:], in0=rs[:], scalar=1.0, in1=var[:], op0=ALU.add, op1=ALU.mult)
-            nc.scalar.activation(out=inv_win[t][:, :V], in_=quarter[:], func=ACT.Abs_reciprocal_sqrt, scale=4.0, bias=1.0)
+            nc.scalar.activation(out=rs[:], in_=var[:], func=ACT.Abs_reciprocal_sqrt, bias=0.1)
+            root = ring.tile([P, V], F32, name="root")
+            nc.vector.scalar_tensor_tensor(out=root[:], in0=var[:], scalar=0.1, in1=rs[:], op0=ALU.add, op1=ALU.mult)
+            for h in range(HALVES):
+                turned_sum(spread[t][:, 1, block(h)], [var[:, block(h)], root[:, block(h)]])
+            nc.scalar.activation(out=inv_win[t][:, :V], in_=spread[t][:, 1, :], func=ACT.Abs_reciprocal_sqrt, scale=4.0, bias=1.4)
 
-        def scale(t):
-            for c in range(2):
-                cols = slice(c * half, (c + 1) * half)
-                inv = ring.tile([P, half], F32, name="inv", bufs=INVB)
-                look_up(INV[2 * t + c], inv[:], inv_win[t], c)
-                nc.vector.scalar_tensor_tensor(
-                    out=hid[c][:, t, :], in0=mix[t][:, cols], scalar=unit_t[:, t : t + 1], in1=inv[:], op0=ALU.mult, op1=ALU.mult
-                )
+        def blend(t, n):
+            part = sb("part%d" % t, [P, U], F32)[:] if AFTER[n] < 0 else feat[units[AFTER[n]]][:].rearrange("p d v -> p (d v)")
+            if MN[n] == "F":
+                nc.vector.tensor_tensor(part, agg_win[t][:].indirect(new_t[:]), cold2[:, t, :], ALU.mult)
+            else:
+                nc.scalar.activation(part, agg_win[t][:].indirect(new_t[:]), ACT.Copy)
+                pick(PART[n]).tensor_tensor(out=part, in0=part, in1=cold2[:, t, :], op=ALU.mult)
+            pick(MIX[n]).tensor_tensor(out=mix[:, t, :], in0=part, in1=own2[:, t, :], op=ALU.add)
 
-        for t in range(PACK):
-            centre(t)
+        def look(t, n, c):
+            entries = new_t[:, c * half // 16 : (c + 1) * half // 16]
+            if INV[2 * n + c] == "S":
+                nc.scalar.activation(looked[c][:, t, :], inv_win[t][:].indirect(entries), ACT.Copy)
+            else:
+                nc.vector.tensor_copy(looked[c][:, t, :], inv_win[t][:].indirect(entries))
+
+        order = [0, 1, 2, 3]
+        centre(CEN)
+        centre(1 - CEN)
         if ORD == 0:
-            for t in range(EARLY):
-                blend(t)
-            for t in range(PACK):
+            for t in order:
                 deviate(t)
-            for t in range(PACK):
-                spread_sum(t)
+            for n, t in enumerate(order):
+                spread_sum(t, n)
                 finish(t)
-            for t in range(EARLY, PACK):
-                blend(t)
-            for t in range(PACK):
-                scale(t)
+            for n, t in enumerate(order):
+                look(t, n, 0)
+                look(t, n, 1)
+            for n, t in enumerate(order):
+                blend(t, n)
         if ORD == 1:
-            for t in range(PACK):
-                deviate(t)
-                if t < EARLY:
-                    blend(t)
-            for t in range(PACK):
-                spread_sum(t)
-                finish(t)
-            for t in range(EARLY, PACK):
-                blend(t)
-            for t in range(PACK):
-                scale(t)
+            for n in range(PACK + 2):
+                if n < PACK:
+                    deviate(order[n])
+                if 0 <= n - 1 < PACK:
+                    spread_sum(order[n - 1], n - 1)
+                if 0 <= n - 2 < PACK:
+                    finish(order[n - 2])
+            for n, t in enumerate(order):
+                blend(t, n)
+            for n, t in enumerate(order):
+                look(t, n, 0)
+                look(t, n, 1)
         if ORD == 2:
-            for t in range(PACK):
+            for t in order:
                 deviate(t)
-                if t < EARLY:
-                    blend(t)
-            for t in range(PACK + 1):
-                if t < PACK:
-                    spread_sum(t)
-                if t > 0:
-                    finish(t - 1)
-            for t in range(PACK):
-                if t >= EARLY:
-                    blend(t)
-                scale(t)
-        if ORD == 3:
-            for t in range(PACK + 2):
-                if t < PACK:
-                    deviate(t)
-                if t < EARLY:
-                    blend(t)
-                if 0 <= t - 1 < PACK:
-                    spread_sum(t - 1)
-                if 0 <= t - 2 < PACK:
-                    finish(t - 2)
-            for t in range(PACK):
-                if t >= EARLY:
-                    blend(t)
-                scale(t)
+            for n, t in enumerate(order):
+                spread_sum(t, n)
+                finish(t)
+            for n, t in enumerate(order):
+                blend(t, n)
+            for c in range(2):
+                for n, t in enumerate(order):
+                    look(t, n, c)
 
         for c in range(2):
             cols = slice(c * half, (c + 1) * half)
             woven = sb("woven%d" % c, [P, half, PACK], BF16)
-            if WEAVE[c] == "V":
-                nc.vector.tensor_copy(out=woven[:], in_=hid[c][:].rearrange("p t r -> p r t"))
-            else:
-                nc.scalar.copy(out=woven[:], in_=hid[c][:].rearrange("p t r -> p r t"))
+            nc.vector.tensor_tensor(
+                out=woven[:].rearrange("p (g i) t -> p g t i", i=4),
+                in0=mix[:, :, cols].rearrange("p t (g i) -> p g t i", i=4),
+                in1=looked[c][:].rearrange("p t (g i) -> p g t i", i=4),
+                op=ALU.mult,
+            )
             codes = sb("codes%d" % c, [P, half], U32)
             scales = sb("scales%d" % c, [P, half], U8)
             nc.vector.quantize_mx(out=codes[:].bitcast(FP8X4), scales=scales[:], in_=woven[:].rearrange("p r t -> p (r t)"))
-            bank = big.tile([P, 2, half], F32, name="bank")
             for m in range(N // P):
+                bank = big.tile([P, P, D], F32, name="bank")
+                rows = bank[:].rearrange("p v d -> p (v d)")[:, :half]
                 nc.tensor.matmul_mx(
-                    out=bank[:, m, :],
+                    out=rows,
                     lhsT=w3w[:, 2 * P * m : 2 * P * (m + 1)].bitcast(FP4X4),
                     lhsT_scale=w3s[:, P * m : P * (m + 1)],
                     rhs=codes[:].bitcast(FP8X4),
@@ -356,6 +339,9 @@ def tile_picked_ycoldb_rel_p_kernel(
                     start=True,
                     stop=True,
                 )
-            res = sb("res%d" % c, [P, 2, half], F32)
-            nc.scalar.copy(out=res[:], in_=bank[:])
-            nc.sync.dma_start(out=out[:, cols].rearrange("(m p) r -> p m r", p=P), in_=res[:])
+                res = sb("res%d%d" % (c, m), [P, half], F32)
+                if RES[m] == "S":
+                    nc.scalar.copy(out=res[:], in_=rows)
+                else:
+                    nc.vector.tensor_copy(out=res[:], in_=rows)
+                (nc.sync if m == 0 else nc.scalar).dma_start(out=out[block(m), cols], in_=res[:])

@@ -78,50 +78,45 @@ def tile_picked_ycoldb_rel_p_kernel(
         new_t = sb("new_t", [P, U // 16], U16)
         xw = sb("xw", [P, T], U32)
         xs = sb("xs", [P, T], U8)
-        w_raw = [sb("w_raw0", [P, 2 * H], U8, tag="w3w"), sb("w_raw1", [P, 2 * H], U8, tag="cnt_t")]
-        ws_raw = [sb("ws_raw0", [P, H], U8), sb("ws_raw1", [P, H], U8, tag="idv_t")]
+        w_raw = [sb("w_raw0", [P, 2 * H], U8, tag="cnt_t"), sb("w_raw1", [P, 2 * H], U8, tag="idv_t")]
+        ws_raw = sb("ws_raw1", [P, H], U8, tag="picked1")
         w_words = [sb("w_words%d" % a, [P, 2 * H], U8) for a in range(2)]
         w_scales = [sb("w_scales%d" % a, [P, H], U8) for a in range(2)]
-        w3s = sb("w3s", [P, N], U8)
         unit_t = sb("unit_t", [P, PACK], F32)
         ident = sb("ident", [P, P], F32)
 
         nc.vector.memset(xs[:].bitcast(I32), 0)
-        nc.vector.memset(ws_raw[1][:].bitcast(I32), 0)
+        nc.vector.memset(ws_raw[:].bitcast(I32), 0)
         nc.sync.dma_start(offs_t[:], offs)
         nc.sync.dma_start(new_t[:], new)
         nc.sync.dma_start(out=w_raw[1][:].bitcast(I32), in_=w2_words[0].bitcast(I32))
         nc.sync.dma_start(out=xw[:].bitcast(I32), in_=x_words[0].rearrange("p c r -> p (c r)").bitcast(I32))
         load_scales([nc.scalar] * 4, xs, x_scales[0])
-        load_scales([nc.gpsimd, nc.scalar, nc.scalar, nc.scalar], ws_raw[1], w2_scales[0])
-        nc.vector.memset(ws_raw[0][:].bitcast(I32), 0)
-        nc.vector.memset(w3s[:].bitcast(I32), 0)
+        load_scales([nc.gpsimd, nc.gpsimd, nc.sync, nc.sync], ws_raw, w2_scales[0])
         deal_words(nc, w_words[1], w_raw[1])
-        deal_scales(nc.gpsimd, w_scales[1], ws_raw[1])
         nc.gpsimd.dma_start(out=w_raw[0][:].bitcast(I32), in_=w1_words[0].bitcast(I32))
-        nc.gpsimd.dma_start(out=unit_t[:], in_=unit.rearrange("(p t) o -> p (t o)", t=PACK))
         make_identity(nc, ident[:])
+        nc.gpsimd.dma_start(out=unit_t[:], in_=unit.rearrange("(p t) o -> p (t o)", t=PACK))
 
         x_cols = S // HALVES
-        xq_scales = [sb("xq_scales%d" % h, [P, x_cols], U8)[:] for h in range(HALVES)]
+        picked_scales = sb("picked_scales", [P, S], U8)
+        xq_scales = [picked_scales[:, h * x_cols : (h + 1) * x_cols] for h in range(HALVES)]
 
         def gather(dst, table, h):
             nc.vector.tensor_copy(dst[h], table[:].indirect(offs_t[:, h * x_cols // 16 : (h + 1) * x_cols // 16]))
 
-        for h in range(HALVES):
-            gather(xq_scales, xs, h)
-        picked = sb("picked", [P, HALVES, x_cols], U32, tag="xs")
-        xq_words = [picked[:, h, :] for h in range(HALVES)]
-        cnt_t = sb("cnt_t", [P, PACK, U], F32)
-        idv_t = sb("idv_t", [P, PACK, U], F32)
-        nc.sync.dma_start(out=cnt_t[:], in_=cnt.rearrange("(p t) r -> p t r", t=PACK))
-        load_scales([nc.sync] * 4, ws_raw[0], w1_scales[0])
-        nc.sync.dma_start(out=idv_t[:], in_=idv.rearrange("(p t) r -> p t r", t=PACK))
+        nc.vector.tensor_copy(picked_scales[:], xs[:].indirect(offs_t[:]))
+        deal_scales(nc.vector, w_scales[1], ws_raw)
+        xq_words = [sb("picked0", [P, x_cols], U32, tag="xs")[:], sb("picked1", [P, x_cols], U32)[:]]
         deal_words(nc, w_words[0], w_raw[0])
-        deal_scales(nc.gpsimd, w_scales[0], ws_raw[0])
-        w3w = sb("w3w", [P, 2 * N], U8)
-        nc.sync.dma_start(out=w3w[:].bitcast(I32), in_=w3_words[0].bitcast(I32))
-        load_scales([nc.sync] * 4, w3s, w3_scales[0])
+        cnt_t = sb("cnt_t", [P, PACK, U], F32)
+        nc.sync.dma_start(out=cnt_t[:], in_=cnt.rearrange("(p t) r -> p t r", t=PACK))
+        ws_raw = sb("ws_raw0", [P, H], U8, tag="idv_t")
+        nc.gpsimd.memset(ws_raw[:].bitcast(I32), 0)
+        load_scales([nc.sync] * 4, ws_raw, w1_scales[0])
+        deal_scales(nc.gpsimd, w_scales[0], ws_raw)
+        idv_t = sb("idv_t", [P, PACK, U], F32)
+        nc.sync.dma_start(out=idv_t[:], in_=idv.rearrange("(p t) r -> p t r", t=PACK))
 
         agg_win = [sb("agg_win%d" % t, [P, U + 16], F32) for t in range(PACK)]
         inv_win = [sb("inv_win%d" % t, [P, WINDOW], F32) for t in range(PACK)]
@@ -188,7 +183,7 @@ def tile_picked_ycoldb_rel_p_kernel(
             sum_over_d(first[t // 2][:, t % 2, block(h)], feat[u])
 
         minus_unit = sb("minus_unit", [P, PACK], F32)
-        nc.gpsimd.tensor_scalar(out=minus_unit[:], in0=unit_t[:], scalar1=-1.0, scalar2=0.0, op0=ALU.mult, op1=ALU.add)
+        nc.scalar.activation(out=minus_unit[:], in_=unit_t[:], func=ACT.Copy, scale=-1.0)
         gather(xq_words, xw, 0)
         gather(xq_words, xw, 1)
         squared = sb("squared", [P, PACK, V], F32)
@@ -220,6 +215,11 @@ def tile_picked_ycoldb_rel_p_kernel(
         for u in units[len(early) :]:
             weigh(u)
         half = U // 2
+        w3s = sb("w3s", [P, N], U8, tag="idv_t")
+        nc.gpsimd.memset(w3s[:].bitcast(I32), 0)
+        load_scales([nc.sync] * 4, w3s, w3_scales[0])
+        w3w = sb("w3w", [P, 2 * N], U8, tag="cnt_t")
+        nc.sync.dma_start(out=w3w[:].bitcast(I32), in_=w3_words[0].bitcast(I32))
         looked = [sb("looked%d" % c, [P, PACK, half], F32) for c in range(2)]
         mix = sb("mix", [P, PACK, U], F32)
         spread, square = {}, {}

from contextlib import ExitStack

import concourse.mybir as mybir
from concourse.masks import make_identity

K, T, S, D, N, H, V, U = 512, 4096, 1024, 4, 256, 512, 256, 512
FLOPS = 2 * K * H * S * 2 + 2 * H * N * U

F32 = mybir.dt.float32
BF16 = mybir.dt.bfloat16
I32 = mybir.dt.int32
U32 = mybir.dt.uint32
U16 = mybir.dt.uint16
U8 = mybir.dt.uint8
FP8X4 = mybir.dt.float8_e4m3fn_x4
FP4X4 = mybir.dt.float4_e2m1fn_x4
ALU = mybir.AluOpType
ACT = mybir.ActivationFunctionType
AX = mybir.AxisListType

P = 128
PACK = 4
HALVES = V // P
WINDOW = V + 16
SQE = "GGGGVVVV"
MN = "SSFF"
PART = "VVVV"
MIX = "VVVV"
INV = "SSSSSSSS"
RES = "SV"
XSPLIT = 4
TH = 0
ORD = 1
RING = 3
CEN = 0
EARLY = [2, 3]
SQ = 4
AFTER = [-1, 3, 6, 7]


def load_scales(queues, plane, rows):
    for q, queue in enumerate(queues):
        queue.dma_start(out=plane[32 * q : 32 * q + 4, :].bitcast(I32), in_=rows[4 * q : 4 * q + 4, :].bitcast(I32))


def deal_words(nc, words, raw):
    nc.scalar.copy(
        out=words[:].bitcast(U16).rearrange("p (t m) -> p t m", t=PACK),
        in_=raw[:].bitcast(U16).rearrange("p (m t) -> p t m", t=PACK),
    )


def deal_scales(engine, scales, raw):
    engine.tensor_copy(
        out=scales[:].rearrange("p (t m) -> p t m", t=PACK),
        in_=raw[:].rearrange("p (m t) -> p t m", t=PACK),
    )


def tile_picked_ycoldb_rel_p_kernel(
    tc, x_words, x_scales, w1_words, w1_scales, w2_words, w2_scales, cnt, idv, unit, w3_words, w3_scales, offs, new, out
):
    nc = tc.nc
    with ExitStack() as ctx:
        keep = ctx.enter_context(tc.tile_pool(name="keep", bufs=1))
        ring = ctx.enter_context(tc.tile_pool(name="ring", bufs=RING))
        big = ctx.enter_context(tc.psum_pool(name="big", bufs=3))
        hold = ctx.enter_context(tc.psum_pool(name="hold", bufs=2))
        sum_banks = ctx.enter_context(tc.psum_pool(name="sum_banks", bufs=3))

        def sb(name, shape, dtype, tag=None):
            return keep.tile(shape, dtype, name=name, tag=tag or name, align_bytes=64)

        def pick(letter):
            return nc.vector if letter == "V" else nc.gpsimd

        offs_t = sb("offs_t", [P, S // 16], U16)
        new_t = sb("new_t", [P, U // 16], U16)
        xw = sb("xw", [P, T], U32)
        xs = sb("xs", [P, T], U8)
        w_raw = [sb("w_raw0", [P, 2 * H], U8, tag="cnt_t"), sb("w_raw1", [P, 2 * H], U8, tag="idv_t")]
        ws_raw = sb("ws_raw1", [P, H], U8, tag="picked1")
        w_words = [sb("w_words%d" % a, [P, 2 * H], U8) for a in range(2)]
        w_scales = [sb("w_scales%d" % a, [P, H], U8) for a in range(2)]
        unit_t = sb("unit_t", [P, PACK], F32)
        ident = sb("ident", [P, P], F32)

        nc.vector.memset(xs[:].bitcast(I32), 0)
        nc.vector.memset(ws_raw[:].bitcast(I32), 0)
        nc.sync.dma_start(offs_t[:], offs)
        nc.sync.dma_start(new_t[:], new)
        nc.sync.dma_start(out=w_raw[1][:].bitcast(I32), in_=w2_words[0].bitcast(I32))
        nc.sync.dma_start(out=xw[:].bitcast(I32), in_=x_words[0].rearrange("p c r -> p (c r)").bitcast(I32))
        load_scales([nc.scalar] * 4, xs, x_scales[0])
        load_scales([nc.gpsimd, nc.gpsimd, nc.sync, nc.sync], ws_raw, w2_scales[0])
        deal_words(nc, w_words[1], w_raw[1])
        nc.gpsimd.dma_start(out=w_raw[0][:].bitcast(I32), in_=w1_words[0].bitcast(I32))
        make_identity(nc, ident[:])
        nc.gpsimd.dma_start(out=unit_t[:], in_=unit.rearrange("(p t) o -> p (t o)", t=PACK))

        x_cols = S // HALVES
        picked_scales = sb("picked_scales", [P, S], U8)
        xq_scales = [picked_scales[:, h * x_cols : (h + 1) * x_cols] for h in range(HALVES)]

        def gather(dst, table, h):
            nc.vector.tensor_copy(dst[h], table[:].indirect(offs_t[:, h * x_cols // 16 : (h + 1) * x_cols // 16]))

        nc.vector.tensor_copy(picked_scales[:], xs[:].indirect(offs_t[:]))
        deal_scales(nc.vector, w_scales[1], ws_raw)
        xq_words = [sb("picked0", [P, x_cols], U32, tag="xs")[:], sb("picked1", [P, x_cols], U32)[:]]
        deal_words(nc, w_words[0], w_raw[0])
        cnt_t = sb("cnt_t", [P, PACK, U], F32)
        nc.sync.dma_start(out=cnt_t[:], in_=cnt.rearrange("(p t) r -> p t r", t=PACK))
        ws_raw = sb("ws_raw0", [P, H], U8, tag="idv_t")
        nc.gpsimd.memset(ws_raw[:].bitcast(I32), 0)
        load_scales([nc.sync] * 4, ws_raw, w1_scales[0])
        deal_scales(nc.gpsimd, w_scales[0], ws_raw)
        idv_t = sb("idv_t", [P, PACK, U], F32)
        nc.sync.dma_start(out=idv_t[:], in_=idv.rearrange("(p t) r -> p t r", t=PACK))

        agg_win = [sb("agg_win%d" % t, [P, U + 16], F32) for t in range(PACK)]
        inv_win = [sb("inv_win%d" % t, [P, WINDOW], F32) for t in range(PACK)]
        for t in range(PACK):
            nc.gpsimd.memset(agg_win[t][:, V:], 0.0)
            nc.gpsimd.memset(inv_win[t][:, V:], 0.0)

        def product(a, t, h, pool=big):
            bank = pool.tile([P, P, D], F32, name="bank")
            nc.tensor.matmul_mx(
                out=bank[:].rearrange("p v d -> p (v d)"),
                lhsT=w_words[a][:, 2 * P * t : 2 * P * (t + 1)].bitcast(FP4X4),
                lhsT_scale=w_scales[a][:, P * t : P * (t + 1)],
                rhs=xq_words[h].bitcast(FP8X4),
                rhs_scale=xq_scales[h],
                start=True,
                stop=True,
            )
            return bank

        def planes_of(bank):
            return bank[:].rearrange("p v d -> p d v")

        def turned_sum(dst, terms):
            for n, term in enumerate(terms):
                nc.tensor.matmul(dst, lhsT=term, rhs=ident[:], start=(n == 0), stop=(n == len(terms) - 1), is_transpose=True)

        def sum_over_d(dst, planes):
            turned_sum(dst, [planes[:, d, :] for d in range(D)])

        def over_d(plane):
            return plane.unsqueeze(1).to_broadcast([P, D, P])

        def block(h):
            return slice(h * P, (h + 1) * P)

        units = [(t, h) for t in range(PACK) for h in range(HALVES)]
        total = [sum_banks.tile([P, 2, V], F32, name="sums") for a in range(2)]
        first = {}
        cold2 = sb("cold2", [P, PACK, U], F32)
        own2 = sb("own2", [P, PACK, U], F32)
        expo, score, top, diff, feat, held, th = {}, {}, {}, {}, {}, {}, {}

        def score_max(u):
            score[u] = product(1, *u)
            top[u] = ring.tile([P, P], F32, name="top")
            nc.vector.tensor_reduce(out=top[u][:], in_=score[u][:], axis=AX.X, op=ALU.max)

        def score_exp(u):
            t, h = u
            diff[u] = sb("diff%d%d" % u, [P, D, P], F32)
            nc.vector.tensor_tensor(out=diff[u][:], in0=planes_of(score[u]), in1=over_d(top[u][:]), op=ALU.subtract)
            expo[u] = sb("expo%d%d" % u, [P, D, P], F32)
            nc.scalar.activation(out=expo[u][:], in_=diff[u][:], func=ACT.Exp)
            sum_over_d(total[t // 2][:, t % 2, block(h)], expo[u])

        def weigh(u):
            t, h = u
            if t % 2 == 0 and h == 0:
                first[t // 2] = sum_banks.tile([P, 2, V], F32, name="sums")
            held[u] = product(0, t, h, hold if t == 0 else big)
            feat[u] = sb("feat%d%d" % u, [P, D, P], F32)
            nc.vector.tensor_tensor(out=feat[u][:], in0=planes_of(held[u]), in1=expo[u][:], op=ALU.mult)
            sum_over_d(first[t // 2][:, t % 2, block(h)], feat[u])

        minus_unit = sb("minus_unit", [P, PACK], F32)
        nc.scalar.activation(out=minus_unit[:], in_=unit_t[:], func=ACT.Copy, scale=-1.0)
        gather(xq_words, xw, 0)
        gather(xq_words, xw, 1)
        squared = sb("squared", [P, PACK, V], F32)
        early = EARLY
        score_max(units[0])
        for n, u in enumerate(units):
            if n + 1 < len(units):
                score_max(units[n + 1])
            score_exp(u)
            if n in early:
                weigh(units[early.index(n)])
            if n == SQ:
                nc.scalar.activation(out=squared[:, :2, :], in_=total[0][:], func=ACT.Square)
            if n >= TH and n < TH + PACK:
                t = n - TH
                th[t] = diff[units[n]][:].rearrange("p d v -> p (d v)")
                nc.scalar.activation(out=th[t], in_=cnt_t[:, t, :], func=ACT.Tanh, scale=0.5)
        for t in range(PACK):
            gain = unit_t[:, t : t + 1]
            nc.gpsimd.tensor_scalar(
                out=cold2[:, t, :], in0=th[t], scalar1=minus_unit[:, t : t + 1], scalar2=gain, op0=ALU.mult, op1=ALU.add
            )
            nc.gpsimd.tensor_scalar(out=th[t], in0=th[t], scalar1=gain, scalar2=gain, op0=ALU.mult, op1=ALU.add)
            nc.gpsimd.tensor_tensor(out=own2[:, t, :], in0=th[t], in1=idv_t[:, t, :], op=ALU.mult)
        inv_total = [diff[u][:].rearrange("p (a b) v -> p a (b v)", a=2) for u in (units[-1], units[-2])]
        nc.scalar.activation(out=squared[:, 2:, :], in_=total[1][:], func=ACT.Square)
        for a in range(2):
            nc.scalar.activation(out=inv_total[a], in_=squared[:, 2 * a : 2 * a + 2, :], func=ACT.Abs_reciprocal_sqrt)
        for u in units[len(early) :]:
            weigh(u)
        half = U // 2
        w3s = sb("w3s", [P, N], U8, tag="idv_t")
        nc.gpsimd.memset(w3s[:].bitcast(I32), 0)
        load_scales([nc.sync] * 4, w3s, w3_scales[0])
        w3w = sb("w3w", [P, 2 * N], U8, tag="cnt_t")
        nc.sync.dma_start(out=w3w[:].bitcast(I32), in_=w3_words[0].bitcast(I32))
        looked = [sb("looked%d" % c, [P, PACK, half], F32) for c in range(2)]
        mix = sb("mix", [P, PACK, U], F32)
        spread, square = {}, {}

        def centre(a):
            mean = ring.tile([P, 2, V], F32, name="mean")
            nc.vector.tensor_tensor(out=mean[:], in0=first[a][:], in1=inv_total[a], op=ALU.mult)
            turned = sum_banks.tile([P, 2, V], F32, name="sums")
            for b in range(2):
                for h in range(HALVES):
                    turned_sum(turned[:, b, block(h)], [mean[:, b, block(h)]])
            for b in range(2):
                nc.scalar.copy(out=agg_win[2 * a + b][:, :V], in_=turned[:, b, :])

        def deviate(t):
            for h in range(HALVES):
                bank = held[t, h] if t in (0, 3) else product(0, t, h, big if (t, h) == (2, 0) else hold)
                dev = feat[t, h][:]
                nc.vector.tensor_tensor(out=dev, in0=planes_of(bank), in1=over_d(agg_win[t][:, block(h)]), op=ALU.subtract)
                square[t, h] = sb("square%d%d" % (t, h), [P, D, P], F32)
                nc.scalar.activation(out=square[t, h][:], in_=dev, func=ACT.Square)

        def spread_sum(t, n):
            spread[t] = sum_banks.tile([P, 2, V], F32, name="sums")
            for h in range(HALVES):
                wv = square[t, h]
                pick(SQE[2 * n + h]).tensor_tensor(out=wv[:], in0=wv[:], in1=expo[t, h][:], op=ALU.mult)
                sum_over_d(spread[t][:, 0, block(h)], wv)

        def finish(t):
            var = ring.tile([P, V], F32, name="var")
            nc.vector.tensor_tensor(out=var[:], in0=spread[t][:, 0, :], in1=inv_total[t // 2][:, t % 2, :], op=ALU.mult)
            rs = ring.tile([P, V], F32, name="rs")
            nc.scalar.activation(out=rs[:], in_=var[:], func=ACT.Abs_reciprocal_sqrt, bias=0.1)
            root = ring.tile([P, V], F32, name="root")
            nc.vector.scalar_tensor_tensor(out=root[:], in0=var[:], scalar=0.1, in1=rs[:], op0=ALU.add, op1=ALU.mult)
            for h in range(HALVES):
                turned_sum(spread[t][:, 1, block(h)], [var[:, block(h)], root[:, block(h)]])
            nc.scalar.activation(out=inv_win[t][:, :V], in_=spread[t][:, 1, :], func=ACT.Abs_reciprocal_sqrt, scale=4.0, bias=1.4)

        def blend(t, n):
            part = sb("part%d" % t, [P, U], F32)[:] if AFTER[n] < 0 else feat[units[AFTER[n]]][:].rearrange("p d v -> p (d v)")
            if MN[n] == "F":
                nc.vector.tensor_tensor(part, agg_win[t][:].indirect(new_t[:]), cold2[:, t, :], ALU.mult)
            else:
                nc.scalar.activation(part, agg_win[t][:].indirect(new_t[:]), ACT.Copy)
                pick(PART[n]).tensor_tensor(out=part, in0=part, in1=cold2[:, t, :], op=ALU.mult)
            pick(MIX[n]).tensor_tensor(out=mix[:, t, :], in0=part, in1=own2[:, t, :], op=ALU.add)

        def look(t, n, c):
            entries = new_t[:, c * half // 16 : (c + 1) * half // 16]
            if INV[2 * n + c] == "S":
                nc.scalar.activation(looked[c][:, t, :], inv_win[t][:].indirect(entries), ACT.Copy)
            else:
                nc.vector.tensor_copy(looked[c][:, t, :], inv_win[t][:].indirect(entries))

        order = [0, 1, 2, 3]
        centre(CEN)
        centre(1 - CEN)
        if ORD == 0:
            for t in order:
                deviate(t)
            for n, t in enumerate(order):
                spread_sum(t, n)
                finish(t)
            for n, t in enumerate(order):
                look(t, n, 0)
                look(t, n, 1)
            for n, t in enumerate(order):
                blend(t, n)
        if ORD == 1:
            for n in range(PACK + 2):
                if n < PACK:
                    deviate(order[n])
                if 0 <= n - 1 < PACK:
                    spread_sum(order[n - 1], n - 1)
                if 0 <= n - 2 < PACK:
                    finish(order[n - 2])
            for n, t in enumerate(order):
                blend(t, n)
            for n, t in enumerate(order):
                look(t, n, 0)
                look(t, n, 1)
        if ORD == 2:
            for t in order:
                deviate(t)
            for n, t in enumerate(order):
                spread_sum(t, n)
                finish(t)
            for n, t in enumerate(order):
                blend(t, n)
            for c in range(2):
                for n, t in enumerate(order):
                    look(t, n, c)

        for c in range(2):
            cols = slice(c * half, (c + 1) * half)
            woven = sb("woven%d" % c, [P, half, PACK], BF16)
            nc.vector.tensor_tensor(
                out=woven[:].rearrange("p (g i) t -> p g t i", i=4),
                in0=mix[:, :, cols].rearrange("p t (g i) -> p g t i", i=4),
                in1=looked[c][:].rearrange("p t (g i) -> p g t i", i=4),
                op=ALU.mult,
            )
            codes = sb("codes%d" % c, [P, half], U32)
            scales = sb("scales%d" % c, [P, half], U8)
            nc.vector.quantize_mx(out=codes[:].bitcast(FP8X4), scales=scales[:], in_=woven[:].rearrange("p r t -> p (r t)"))
            for m in range(N // P):
                bank = big.tile([P, P, D], F32, name="bank")
                rows = bank[:].rearrange("p v d -> p (v d)")[:, :half]
                nc.tensor.matmul_mx(
                    out=rows,
                    lhsT=w3w[:, 2 * P * m : 2 * P * (m + 1)].bitcast(FP4X4),
                    lhsT_scale=w3s[:, P * m : P * (m + 1)],
                    rhs=codes[:].bitcast(FP8X4),
                    rhs_scale=scales[:],
                    start=True,
                    stop=True,
                )
                res = sb("res%d%d" % (c, m), [P, half], F32)
                if RES[m] == "S":
                    nc.scalar.copy(out=res[:], in_=rows)
                else:
                    nc.vector.tensor_copy(out=res[:], in_=rows)
                (nc.sync if m == 0 else nc.scalar).dma_start(out=out[block(m), cols], in_=res[:])
